import numpy as np
import ml_dtypes


def mxq(x, axis, fmt="e4m3"):
    dtype, down = {"e4m3": (ml_dtypes.float8_e4m3fn, 7), "e5m2": (ml_dtypes.float8_e5m2, 14)}[fmt]
    v = np.moveaxis(np.asarray(x, np.float32).astype(ml_dtypes.bfloat16).astype(np.float64), axis, -1)
    blocks = v.reshape(v.shape[:-1] + (-1, 32))
    amax = np.abs(blocks).max(-1, keepdims=True)
    byte = np.maximum(np.where(amax > 0, np.frexp(amax)[1] - 1 + 127, 0) - down, 1)
    scale = np.exp2(byte - 127.0)
    codes = (blocks / scale).astype(np.float32).astype(dtype).astype(np.float64)
    return np.moveaxis((codes * scale).reshape(v.shape), -1, axis)


WIDE = False


def mx_kscale(k):
    if not WIDE:
        return np.ones(k)
    levels = np.array([10, -10, 5, -5, 0])
    if k % 512:
        return np.exp2(np.random.permutation(np.resize(levels, k // 32))).repeat(32)
    a = np.empty((k // 512, 16))
    for p in range(k // 512):
        a[p, :8] = np.random.permutation(np.resize(levels, 8))
        for g in range(8):
            far = levels[np.abs(levels - a[p, g]) >= 10]
            a[p, g + 8] = far[np.random.randint(len(far))]
    return np.exp2(a.ravel()).repeat(32)


def f64(x):
    return np.asarray(x).astype(np.float64)


def striped(idx):
    return np.tile(np.asarray(idx).reshape(-1, 16).T, (8, 1)).astype(np.uint16)


def unstriped(offs):
    return offs[:16].T.reshape(-1).astype(np.int64)


def striped8(idx):
    return np.asarray(idx).reshape(8, -1, 16).transpose(0, 2, 1).reshape(128, -1).astype(np.uint16)


def unstriped8(offs):
    return offs.reshape(8, 16, -1).transpose(0, 2, 1).reshape(8, -1).astype(np.int64)


def pick8(x, idx, run):
    r = np.arange(len(x))
    return x[r[:, None], idx[r % (8 * run) // run]]


E2M1 = np.array([0.0, 0.5, 1.0, 1.5, 2.0, 3.0, 4.0, 6.0, -0.0, -0.5, -1.0, -1.5, -2.0, -3.0, -4.0, -6.0])


def pack_weight(w, fmt):
    k, n = w.shape
    w = f64(np.asarray(w, np.float32).astype(ml_dtypes.bfloat16)).reshape(k // 32, 32, n)
    amax = np.abs(w).max(1)
    if fmt == "e4m3":
        byte = np.frexp(amax)[1] - 1 + 127 - 7
    else:
        mant, ex = np.frexp(amax / 6.0)
        byte = np.where(mant > 0.5, ex, ex - 1) + 127
    byte = np.clip(np.where(amax > 0, byte, 1), 1, 254)
    scaled = (w * np.exp2(127.0 - byte)[:, None, :]).reshape(k, n).astype(np.float32)
    by_word = np.ascontiguousarray(scaled.reshape(k // 512, 128, 4, n).transpose(0, 1, 3, 2))
    if fmt == "e4m3":
        words = by_word.astype(ml_dtypes.float8_e4m3fn).view(np.uint8)
    else:
        c = by_word.astype(ml_dtypes.float4_e2m1fn).view(np.uint8) & 0xF
        words = (c[..., 0::2] | (c[..., 1::2] << 4)).reshape(k // 512, 128, 2 * n)
    return np.ascontiguousarray(words), np.ascontiguousarray(byte.astype(np.uint8).reshape(k // 512, 16, n))


def unpack_weight(words, scales, fmt):
    g, _, n = scales.shape
    words = np.ascontiguousarray(words).reshape(g, 128, n, -1)
    if fmt == "e4m3":
        vals = words.view(ml_dtypes.float8_e4m3fn).astype(np.float64)
    else:
        nib = np.empty((g, 128, n, 4), np.uint8)
        nib[..., 0::2] = words & 0xF
        nib[..., 1::2] = words >> 4
        vals = E2M1[nib]
    vals = vals * np.repeat(np.exp2(scales.astype(np.float64) - 127.0), 8, axis=1)[..., None]
    return vals.transpose(0, 1, 3, 2).reshape(g * 512, n)


K, J, R, T, C, O, N, S = 512, 512, 512, 2048, 1024, 512, 256, 1024


def setup_inputs():
    n = np.random.standard_normal
    idx = np.random.permutation(T)[:J]
    idx2 = np.stack([np.random.permutation(C)[:J] for _ in range(8)])
    idx3 = np.stack([np.random.permutation(C)[:J] for _ in range(8)])
    idx4 = np.stack([np.random.permutation(C)[:O] for _ in range(8)])
    idx5 = np.random.permutation(S)[:N]
    fk = mx_kscale(K)
    fr = mx_kscale(R)
    xtp = pack_weight(n((K, T)) * fk[:, None], "e2m1")
    wp = pack_weight(n((K, R)) * 1 / np.sqrt(K) / fk[:, None] * fr, "e4m3")
    w2p = pack_weight(n((K, R)) * 1 / np.sqrt(K) / fk[:, None] * fr, "e4m3")
    vsp = pack_weight(n((R, S)) * 1 / np.sqrt(R) / fr[:, None], "e4m3")
    return {
        "xt_words": xtp[0],
        "xt_scales": xtp[1],
        "w_words": wp[0],
        "w_scales": wp[1],
        "w2_words": w2p[0],
        "w2_scales": w2p[1],
        "sa": (np.random.uniform(0.5, 1.6, (R, 1))).astype(np.float32),
        "vs_words": vsp[0],
        "vs_scales": vsp[1],
        "offs": striped(idx),
        "offs2": striped8(idx2),
        "offs3": striped8(idx3),
        "offs4": striped8(idx4),
        "offs5": striped(idx5),
    }


def reference(xt_words, xt_scales, w_words, w_scales, w2_words, w2_scales, sa, vs_words, vs_scales, offs, offs2, offs3, offs4, offs5):
    idx = unstriped(offs)
    idx2 = unstriped8(offs2)
    idx3 = unstriped8(offs3)
    idx4 = unstriped8(offs4)
    idx5 = unstriped(offs5)
    xtu = unpack_weight(xt_words, xt_scales, "e2m1")
    wu = unpack_weight(w_words, w_scales, "e4m3")
    w2u = unpack_weight(w2_words, w2_scales, "e4m3")
    vsu = unpack_weight(vs_words, vs_scales, "e4m3")
    xtidxg = xtu[:, idx]
    a = wu.T @ xtidxg
    b = w2u.T @ xtidxg
    pw = np.zeros((R, C))
    pw[np.arange(R)[:, None], idx2[np.arange(R) % 512 // 64]] = a
    pv = np.zeros((R, C))
    pv[np.arange(R)[:, None], idx3[np.arange(R) % 512 // 64]] = b
    pg = np.maximum(pw, pv)
    pm = np.mean(pg, axis=1, keepdims=True)
    g1 = np.maximum(pg - pm, 0.0)
    hid = pick8(g1, idx4, 64) * f64(sa)
    vsidx5g = vsu[:, idx5]
    hidq = mxq(hid, 0, "e4m3")
    y = vsidx5g.T @ hidq
    return y

@@ -1,0 +1,215 @@
+from contextlib import ExitStack
+
+import concourse.mybir as mybir
+
+K, J, R, T, C, O, N, S = 512, 512, 512, 2048, 1024, 512, 256, 1024
+FLOPS = 2 * (2 * K * R * J + R * N * O)
+
+F32 = mybir.dt.float32
+BF16 = mybir.dt.bfloat16
+I32 = mybir.dt.int32
+U32 = mybir.dt.uint32
+U16 = mybir.dt.uint16
+U8 = mybir.dt.uint8
+FP8X4 = mybir.dt.float8_e4m3fn_x4
+FP4X4 = mybir.dt.float4_e2m1fn_x4
+ALU = mybir.AluOpType
+COPY = mybir.ActivationFunctionType.Copy
+
+P = 128
+PACK = 4
+QUAD = 32
+HALF = 256
+LIST_ROWS = 16
+
+
+def tile_picked_tokens_plain_twin_aboveaverage_store_plain_kernel(
+    tc, xt_words, xt_scales, w_words, w_scales, w2_words, w2_scales, sa, vs_words, vs_scales,
+    offs, offs2, offs3, offs4, offs5, out,
+):
+    nc = tc.nc
+    with ExitStack() as ctx:
+        lists = ctx.enter_context(tc.tile_pool(name="lists", bufs=1))
+        keep = ctx.enter_context(tc.tile_pool(name="keep", bufs=1))
+        psum = ctx.enter_context(tc.psum_pool(name="psum", bufs=1))
+
+        def load_list(source, name):
+            tile = lists.tile(list(source.shape), U16, name=name)
+            nc.sync.dma_start(tile[:], source)
+            return tile
+
+        def entries(tile, first, count):
+            return tile[:, first // LIST_ROWS : (first + count) // LIST_ROWS]
+
+        def load_scale_rows(plane, source):
+            for q in range(P // QUAD):
+                nc.sync.dma_start(
+                    plane[QUAD * q : QUAD * q + PACK, :].bitcast(I32),
+                    source[0, PACK * q : PACK * (q + 1), :].bitcast(I32),
+                )
+
+        def load_weight_scale_rows(plane, source):
+            for u in range(2):
+                rows = source[0, 2 * PACK * u : 2 * PACK * (u + 1), :].rearrange("(q i) c -> i q c", q=2)
+                nc.sync.dma_start(plane[2 * QUAD * u : 2 * QUAD * u + PACK, :, :].bitcast(I32), rows.bitcast(I32))
+
+        def spread_weight_scale_rows(plane):
+            for u in range(2):
+                low = 2 * QUAD * u
+                nc.vector.tensor_copy(
+                    plane[low + QUAD : low + QUAD + PACK, 0, :].bitcast(I32),
+                    plane[low : low + PACK, 1, :].bitcast(I32),
+                )
+
+        def load_words(tile, source):
+            nc.sync.dma_start(tile[:].bitcast(I32), source[0].rearrange("p n t -> p (n t)").bitcast(I32))
+
+        def deal(copy, dealt, raw, first, last):
+            copy(
+                dealt[:, first:last, :].rearrange("p t m -> p m t"),
+                raw.rearrange("p (m t) -> p m t", t=PACK)[:, :, first:last],
+            )
+
+        xs_window = keep.tile([P, T], U8, tag="scale_window", align_bytes=64)
+        nc.vector.memset(xs_window[:].bitcast(I32), 0)
+        ws_raw = keep.tile([P, 2, R], U8, tag="weight_scales_raw", align_bytes=64)
+        nc.vector.memset(ws_raw[:, 0, :].bitcast(I32), 0)
+        token_list = load_list(offs, "token_list")
+        load_scale_rows(xs_window, xt_scales)
+        load_weight_scale_rows(ws_raw, w_scales)
+        xw_window = keep.tile([P, T], U16, tag="word_window", align_bytes=64)
+        nc.sync.dma_start(xw_window[:].bitcast(I32), xt_words[0].bitcast(I32))
+        ww_raw = keep.tile([P, R], U32, tag="weight_words_raw", align_bytes=64)
+        load_words(ww_raw, w_words)
+        board_lists = [load_list(offs2, "first_board_list"), load_list(offs3, "second_board_list")]
+        place_list = load_list(offs4, "place_list")
+        store_list = load_list(offs5, "store_list")
+        sa_tile = keep.tile([P, PACK], F32)
+        nc.sync.dma_start(sa_tile[:], sa.rearrange("(p t) o -> p (t o)", t=PACK))
+
+        first_boards = [keep.tile([P, C], F32, name=f"first_board{i}") for i in range(2)]
+        second_board = keep.tile([P, C], F32)
+        nc.vector.memset(first_boards[0][:], 0.0)
+        nc.vector.memset(second_board[:], 0.0)
+
+        words = [keep.tile([P, PACK, P], U32, name=f"dealt_words{i}", align_bytes=64) for i in range(2)]
+        scales = [keep.tile([P, PACK, P], U8, name=f"dealt_scales{i}", align_bytes=64) for i in range(2)]
+        xw = keep.tile([P, J], U16, align_bytes=64)
+        xs = keep.tile([P, J], U8, align_bytes=64)
+
+        def gather_tokens(first):
+            cols = slice(first, first + HALF)
+            nc.vector.tensor_copy(xs[:, cols], xs_window[:].indirect(entries(token_list, first, HALF)))
+            nc.vector.tensor_copy(xw[:, cols], xw_window[:].indirect(entries(token_list, first, HALF)))
+
+        def product(matrix, t, cols, bank, staged, copy):
+            width = cols.stop - cols.start
+            acc = psum.tile([P, J], F32, tag=f"bank{bank}", name="acc")
+            nc.tensor.matmul_mx(
+                out=acc[:, :width],
+                lhsT=words[matrix][:, t, :].bitcast(FP8X4),
+                lhsT_scale=scales[matrix][:, t, :],
+                rhs=xw[:, cols].bitcast(FP4X4),
+                rhs_scale=xs[:, cols],
+                start=True,
+                stop=True,
+            )
+            copy(staged[:, cols], acc[:, :width])
+
+        staged = {}
+        for t in range(PACK):
+            for matrix in range(2):
+                staged[matrix, t] = keep.tile([P, J], F32, tag=f"staged{matrix}{t}", name="staged", align_bytes=64)
+
+        spread_weight_scale_rows(ws_raw)
+        deal(nc.scalar.copy, words[0], ww_raw[:], 0, 1)
+        deal(nc.vector.tensor_copy, scales[0], ws_raw[:, 0, :], 0, 1)
+        gather_tokens(0)
+        product(0, 0, slice(0, HALF), 0, staged[0, 0], nc.scalar.copy)
+        deal(nc.scalar.copy, words[0], ww_raw[:], 1, PACK)
+        gather_tokens(HALF)
+        product(0, 0, slice(HALF, J), 1, staged[0, 0], nc.vector.tensor_copy)
+        deal(nc.vector.tensor_copy, scales[0], ws_raw[:, 0, :], 1, PACK)
+
+        w2s_raw = keep.tile([P, 2, R], U8, align_bytes=64)
+        nc.vector.memset(w2s_raw[:, 0, :].bitcast(I32), 0)
+        load_weight_scale_rows(w2s_raw, w2_scales)
+        w2w_raw = keep.tile([P, R], U32, tag="weight_words_raw", align_bytes=64)
+        load_words(w2w_raw, w2_words)
+        spread_weight_scale_rows(w2s_raw)
+        deal(nc.vector.tensor_copy, scales[1], w2s_raw[:, 0, :], 0, PACK)
+        deal(nc.vector.tensor_copy, words[1], w2w_raw[:], 0, PACK)
+        product(1, 0, slice(0, J), 2, staged[1, 0], nc.vector.tensor_copy)
+        nc.vector.memset(first_boards[1][:], 0.0)
+        for t in range(1, PACK):
+            for matrix in range(2):
+                product(matrix, t, slice(0, J), (2 * t + matrix + 1) % 8, staged[matrix, t], nc.vector.tensor_copy)
+
+        vs_scale_window = keep.tile([P, S], U8, tag="scale_window", align_bytes=64)
+        nc.vector.memset(vs_scale_window[:].bitcast(I32), 0)
+        load_scale_rows(vs_scale_window, vs_scales)
+        vs_word_window = keep.tile([P, S], U32, tag="word_window", align_bytes=64)
+        load_words(vs_word_window, vs_words)
+        vw = keep.tile([P, N], U32, align_bytes=64)
+        vsc = keep.tile([P, N], U8, align_bytes=64)
+        nc.vector.tensor_copy(vw[:], vs_word_window[:].indirect(store_list[:]))
+        nc.vector.tensor_copy(vsc[:], vs_scale_window[:].indirect(store_list[:]))
+
+        above = []
+        for t in range(PACK):
+            first_board = first_boards[t % 2]
+            pieces = [(0, HALF), (HALF, HALF)] if t == 0 else [(0, J)]
+            for first, count in pieces:
+                nc.scalar.activation(
+                    first_board[:].indirect(entries(board_lists[0], first, count)),
+                    staged[0, t][:, first : first + count],
+                    COPY,
+                )
+            nc.scalar.activation(second_board[:].indirect(board_lists[1][:]), staged[1, t][:], COPY)
+            larger = keep.tile([P, C], F32, tag="larger", name="larger")
+            total = keep.tile([P, 1], F32, tag=f"total{t}", name="total")
+            nc.vector.scalar_tensor_tensor(
+                larger[:], first_board[:], 1.0, second_board[:], ALU.mult, ALU.max, accum_out=total[:]
+            )
+            mean = keep.tile([P, 1], F32, tag=f"mean{t}", name="mean")
+            nc.vector.tensor_scalar(mean[:], total[:], 1.0 / C, None, ALU.mult)
+            excess = keep.tile([P, C], F32, tag=f"excess{t}", name="excess")
+            nc.vector.tensor_scalar(excess[:], larger[:], mean[:], 0.0, ALU.subtract, ALU.max)
+            above.append(excess)
+
+        hid = keep.tile([P, 2, PACK, HALF], BF16, tag=f"staged1{PACK - 1}", align_bytes=64)
+        for h in range(2):
+            for t in range(PACK):
+                nc.scalar.activation(
+                    hid[:, h, t, :],
+                    above[t][:].indirect(entries(place_list, h * HALF, HALF)),
+                    COPY,
+                    scale=sa_tile[:, t : t + 1],
+                )
+        for h in range(2):
+            grouped = keep.tile([P, HALF, PACK], BF16, tag=f"grouped{h}", name="grouped", align_bytes=64)
+            nc.vector.tensor_copy(
+                grouped[:].rearrange("p (c i) t -> p c t i", i=4),
+                hid[:, h, :, :].rearrange("p t (c i) -> p c t i", i=4),
+            )
+            codes = keep.tile([P, HALF], U32, tag=f"codes{h}", name="codes", align_bytes=64)
+            code_scales = keep.tile([P, HALF], U8, tag=f"code_scales{h}", name="code_scales", align_bytes=64)
+            nc.vector.quantize_mx(
+                out=codes[:].bitcast(FP8X4), scales=code_scales[:], in_=grouped[:].rearrange("p c t -> p (c t)")
+            )
+            for b in range(N // P):
+                rows = slice(b * P, (b + 1) * P)
+                acc = psum.tile([P, J], F32, tag=f"bank{2 * h + b + 1}", name="acc")
+                nc.tensor.matmul_mx(
+                    out=acc[:, :HALF],
+                    lhsT=vw[:, rows].bitcast(FP8X4),
+                    lhsT_scale=vsc[:, rows],
+                    rhs=codes[:].bitcast(FP8X4),
+                    rhs_scale=code_scales[:],
+                    start=True,
+                    stop=True,
+                )
+                result = keep.tile([P, HALF], F32, tag=f"result{h}{b}", name="result")
+                copy = nc.scalar.copy if b == 0 else nc.vector.tensor_copy
+                copy(result[:], acc[:, :HALF])
+                nc.sync.dma_start(out[rows, h * HALF : (h + 1) * HALF], result[:])

@@ -21,6 +21,7 @@ PACK = 4
 QUAD = 32
 HALF = 256
 LIST_ROWS = 16
+XW1 = HALF - 32
 
 
 def tile_picked_tokens_plain_twin_aboveaverage_store_plain_kernel(
@@ -48,23 +49,16 @@ def tile_picked_tokens_plain_twin_aboveaverage_store_plain_kernel(
                     source[0, PACK * q : PACK * (q + 1), :].bitcast(I32),
                 )
 
-        def load_weight_scale_rows(plane, source):
-            for u in range(2):
-                rows = source[0, 2 * PACK * u : 2 * PACK * (u + 1), :].rearrange("(q i) c -> i q c", q=2)
-                nc.sync.dma_start(plane[2 * QUAD * u : 2 * QUAD * u + PACK, :, :].bitcast(I32), rows.bitcast(I32))
-
-        def spread_weight_scale_rows(plane):
-            for u in range(2):
-                low = 2 * QUAD * u
+        def spread_scale_rows(plane, rows):
+            for q in range(P // QUAD):
                 nc.vector.tensor_copy(
-                    plane[low + QUAD : low + QUAD + PACK, 0, :].bitcast(I32),
-                    plane[low : low + PACK, 1, :].bitcast(I32),
+                    plane[QUAD * q : QUAD * q + PACK, :].bitcast(I32), rows[0:PACK, q, :].bitcast(I32)
                 )
 
         def load_words(tile, source):
             nc.sync.dma_start(tile[:].bitcast(I32), source[0].rearrange("p n t -> p (n t)").bitcast(I32))
 
-        def deal(copy, dealt, raw, first, last):
+        def deal(copy, dealt, raw, first=0, last=PACK):
             copy(
                 dealt[:, first:last, :].rearrange("p t m -> p m t"),
                 raw.rearrange("p (m t) -> p m t", t=PACK)[:, :, first:last],
@@ -72,35 +66,39 @@ def tile_picked_tokens_plain_twin_aboveaverage_store_plain_kernel(
 
         xs_window = keep.tile([P, T], U8, tag="scale_window", align_bytes=64)
         nc.vector.memset(xs_window[:].bitcast(I32), 0)
-        ws_raw = keep.tile([P, 2, R], U8, tag="weight_scales_raw", align_bytes=64)
-        nc.vector.memset(ws_raw[:, 0, :].bitcast(I32), 0)
         token_list = load_list(offs, "token_list")
-        load_scale_rows(xs_window, xt_scales)
-        load_weight_scale_rows(ws_raw, w_scales)
-        xw_window = keep.tile([P, T], U16, tag="word_window", align_bytes=64)
+        ws_rows = keep.tile([PACK, P // QUAD, R], U8, tag="early_rows", align_bytes=64)
+        nc.sync.dma_start(
+            ws_rows[:].bitcast(I32), w_scales[0].rearrange("(q i) c -> i q c", i=PACK).bitcast(I32)
+        )
+        xw_window = keep.tile([P, T], U16, tag="token_words", align_bytes=64)
         nc.sync.dma_start(xw_window[:].bitcast(I32), xt_words[0].bitcast(I32))
+        load_scale_rows(xs_window, xt_scales)
         ww_raw = keep.tile([P, R], U32, tag="weight_words_raw", align_bytes=64)
         load_words(ww_raw, w_words)
-        board_lists = [load_list(offs2, "first_board_list"), load_list(offs3, "second_board_list")]
+        ws_raw = keep.tile([P, R], U8, align_bytes=64)
+        nc.vector.memset(ws_raw[:].bitcast(I32), 0)
+        w2s_raw = keep.tile([P, R], U8, tag="second_scales", align_bytes=64)
+        nc.vector.memset(w2s_raw[:].bitcast(I32), 0)
+        first_list = load_list(offs2, "first_board_list")
+        load_scale_rows(w2s_raw, w2_scales)
+        board_lists = [first_list, load_list(offs3, "second_board_list")]
         place_list = load_list(offs4, "place_list")
         store_list = load_list(offs5, "store_list")
         sa_tile = keep.tile([P, PACK], F32)
         nc.sync.dma_start(sa_tile[:], sa.rearrange("(p t) o -> p (t o)", t=PACK))
 
         first_boards = [keep.tile([P, C], F32, name=f"first_board{i}") for i in range(2)]
-        second_board = keep.tile([P, C], F32)
-        nc.vector.memset(first_boards[0][:], 0.0)
-        nc.vector.memset(second_board[:], 0.0)
+        for board in first_boards:
+            nc.vector.memset(board[:].bitcast(I32), 0)
 
         words = [keep.tile([P, PACK, P], U32, name=f"dealt_words{i}", align_bytes=64) for i in range(2)]
         scales = [keep.tile([P, PACK, P], U8, name=f"dealt_scales{i}", align_bytes=64) for i in range(2)]
         xw = keep.tile([P, J], U16, align_bytes=64)
         xs = keep.tile([P, J], U8, align_bytes=64)
 
-        def gather_tokens(first):
-            cols = slice(first, first + HALF)
-            nc.vector.tensor_copy(xs[:, cols], xs_window[:].indirect(entries(token_list, first, HALF)))
-            nc.vector.tensor_copy(xw[:, cols], xw_window[:].indirect(entries(token_list, first, HALF)))
+        def gather(dst, window, offsets, first, last):
+            nc.vector.tensor_copy(dst[:, first:last], window[:].indirect(entries(offsets, first, last - first)))
 
         def product(matrix, t, cols, bank, staged, copy):
             width = cols.stop - cols.start
@@ -121,82 +119,96 @@ def tile_picked_tokens_plain_twin_aboveaverage_store_plain_kernel(
             for matrix in range(2):
                 staged[matrix, t] = keep.tile([P, J], F32, tag=f"staged{matrix}{t}", name="staged", align_bytes=64)
 
-        spread_weight_scale_rows(ws_raw)
+        spread_scale_rows(ws_raw, ws_rows)
+        w2w_raw = keep.tile([P, R], U32, tag="early_rows", align_bytes=64)
+        load_words(w2w_raw, w2_words)
+        deal(nc.vector.tensor_copy, scales[0], ws_raw[:])
         deal(nc.scalar.copy, words[0], ww_raw[:], 0, 1)
-        deal(nc.vector.tensor_copy, scales[0], ws_raw[:, 0, :], 0, 1)
-        gather_tokens(0)
+        gather(xw, xw_window, token_list, 0, HALF)
+        gather(xs, xs_window, token_list, 0, HALF)
         product(0, 0, slice(0, HALF), 0, staged[0, 0], nc.scalar.copy)
         deal(nc.scalar.copy, words[0], ww_raw[:], 1, PACK)
-        gather_tokens(HALF)
+        gather(xs, xs_window, token_list, HALF, J)
+        gather(xw, xw_window, token_list, XW1, J)
         product(0, 0, slice(HALF, J), 1, staged[0, 0], nc.vector.tensor_copy)
-        deal(nc.vector.tensor_copy, scales[0], ws_raw[:, 0, :], 1, PACK)
-
-        w2s_raw = keep.tile([P, 2, R], U8, align_bytes=64)
-        nc.vector.memset(w2s_raw[:, 0, :].bitcast(I32), 0)
-        load_weight_scale_rows(w2s_raw, w2_scales)
-        w2w_raw = keep.tile([P, R], U32, tag="weight_words_raw", align_bytes=64)
-        load_words(w2w_raw, w2_words)
-        spread_weight_scale_rows(w2s_raw)
-        deal(nc.vector.tensor_copy, scales[1], w2s_raw[:, 0, :], 0, PACK)
-        deal(nc.vector.tensor_copy, words[1], w2w_raw[:], 0, PACK)
-        product(1, 0, slice(0, J), 2, staged[1, 0], nc.vector.tensor_copy)
-        nc.vector.memset(first_boards[1][:], 0.0)
         for t in range(1, PACK):
-            for matrix in range(2):
-                product(matrix, t, slice(0, J), (2 * t + matrix + 1) % 8, staged[matrix, t], nc.vector.tensor_copy)
+            product(0, t, slice(0, J), 1 + t, staged[0, t], nc.vector.tensor_copy)
+        deal(nc.vector.tensor_copy, scales[1], w2s_raw[:])
+        deal(nc.vector.tensor_copy, words[1], w2w_raw[:])
+        second_boards = [
+            keep.tile([P, C], F32, tag=tag, name="second_board", align_bytes=64)
+            for tag in ("early_rows", "second_scales")
+        ]
+        nc.vector.memset(second_boards[0][:].bitcast(I32), 0)
+        for t in range(PACK):
+            product(1, t, slice(0, J), (5 + t) % 8, staged[1, t], nc.vector.tensor_copy)
+        nc.vector.memset(second_boards[1][:].bitcast(I32), 0)
 
-        vs_scale_window = keep.tile([P, S], U8, tag="scale_window", align_bytes=64)
+        vs_scale_window = keep.tile([P, S], U8, tag="token_words", align_bytes=64)
         nc.vector.memset(vs_scale_window[:].bitcast(I32), 0)
         load_scale_rows(vs_scale_window, vs_scales)
-        vs_word_window = keep.tile([P, S], U32, tag="word_window", align_bytes=64)
+        vs_word_window = keep.tile([P, S], U32, tag="weight_words_raw", align_bytes=64)
         load_words(vs_word_window, vs_words)
         vw = keep.tile([P, N], U32, align_bytes=64)
         vsc = keep.tile([P, N], U8, align_bytes=64)
         nc.vector.tensor_copy(vw[:], vs_word_window[:].indirect(store_list[:]))
         nc.vector.tensor_copy(vsc[:], vs_scale_window[:].indirect(store_list[:]))
 
-        above = []
-        for t in range(PACK):
-            first_board = first_boards[t % 2]
-            pieces = [(0, HALF), (HALF, HALF)] if t == 0 else [(0, J)]
-            for first, count in pieces:
-                nc.scalar.activation(
-                    first_board[:].indirect(entries(board_lists[0], first, count)),
-                    staged[0, t][:, first : first + count],
-                    COPY,
-                )
-            nc.scalar.activation(second_board[:].indirect(board_lists[1][:]), staged[1, t][:], COPY)
-            larger = keep.tile([P, C], F32, tag="larger", name="larger")
+        def scatter(board, offsets, values, first, last):
+            nc.scalar.activation(board[:].indirect(entries(offsets, first, last - first)), values[:, first:last], COPY)
+
+        def compare(t):
+            larger = keep.tile([P, C], F32, tag="larger", name="larger", align_bytes=64)
             total = keep.tile([P, 1], F32, tag=f"total{t}", name="total")
             nc.vector.scalar_tensor_tensor(
-                larger[:], first_board[:], 1.0, second_board[:], ALU.mult, ALU.max, accum_out=total[:]
+                larger[:], first_boards[t % 2][:], 1.0, second_boards[t % 2][:], ALU.mult, ALU.max, accum_out=total[:]
             )
-            mean = keep.tile([P, 1], F32, tag=f"mean{t}", name="mean")
+            mean = keep.tile([P, 1], F32, tag=f"mean{t}", name="mean", align_bytes=64)
             nc.vector.tensor_scalar(mean[:], total[:], 1.0 / C, None, ALU.mult)
             excess = keep.tile([P, C], F32, tag=f"excess{t}", name="excess")
             nc.vector.tensor_scalar(excess[:], larger[:], mean[:], 0.0, ALU.subtract, ALU.max)
-            above.append(excess)
+            return excess
 
-        hid = keep.tile([P, 2, PACK, HALF], BF16, tag=f"staged1{PACK - 1}", align_bytes=64)
-        for h in range(2):
-            for t in range(PACK):
-                nc.scalar.activation(
-                    hid[:, h, t, :],
-                    above[t][:].indirect(entries(place_list, h * HALF, HALF)),
-                    COPY,
-                    scale=sa_tile[:, t : t + 1],
-                )
-        for h in range(2):
-            grouped = keep.tile([P, HALF, PACK], BF16, tag=f"grouped{h}", name="grouped", align_bytes=64)
-            nc.vector.tensor_copy(
-                grouped[:].rearrange("p (c i) t -> p c t i", i=4),
-                hid[:, h, :, :].rearrange("p t (c i) -> p c t i", i=4),
+        scatter(first_boards[0], board_lists[0], staged[0, 0], 0, HALF)
+        scatter(first_boards[0], board_lists[0], staged[0, 0], HALF, J)
+        scatter(first_boards[1], board_lists[0], staged[0, 1], 0, J)
+        above = []
+        for t in range(PACK):
+            if t >= 2:
+                scatter(first_boards[t % 2], board_lists[0], staged[0, t], 0, J)
+            scatter(second_boards[t % 2], board_lists[1], staged[1, t], 0, J)
+            above.append(compare(t))
+
+        last = PACK - 1
+        early = keep.tile([P, PACK + 1, HALF], BF16, tag=f"staged1{last}", align_bytes=64)
+        late = keep.tile([P, last, HALF], BF16, tag="larger", align_bytes=64)
+
+        def fetch(dst, t, h):
+            nc.scalar.activation(
+                dst, above[t][:].indirect(entries(place_list, h * HALF, HALF)), COPY, scale=sa_tile[:, t : t + 1]
             )
+
+        for t in range(last):
+            fetch(early[:, t, :], t, 0)
+        fetch(early[:, PACK, :], 0, 1)
+        fetch(early[:, last, :], last, 0)
+        for t in range(1, PACK):
+            fetch(late[:, t - 1, :], t, 1)
+
+        grouped = [
+            keep.tile([P, HALF, PACK], BF16, tag=tag, name="grouped", align_bytes=64)
+            for tag in ("grouped", f"mean{last}")
+        ]
+
+        def quantise(h):
             codes = keep.tile([P, HALF], U32, tag=f"codes{h}", name="codes", align_bytes=64)
             code_scales = keep.tile([P, HALF], U8, tag=f"code_scales{h}", name="code_scales", align_bytes=64)
             nc.vector.quantize_mx(
-                out=codes[:].bitcast(FP8X4), scales=code_scales[:], in_=grouped[:].rearrange("p c t -> p (c t)")
+                out=codes[:].bitcast(FP8X4), scales=code_scales[:], in_=grouped[h][:].rearrange("p c t -> p (c t)")
             )
+            return codes, code_scales
+
+        def last_product(h, codes, code_scales, copies):
             for b in range(N // P):
                 rows = slice(b * P, (b + 1) * P)
                 acc = psum.tile([P, J], F32, tag=f"bank{2 * h + b + 1}", name="acc")
@@ -210,6 +222,17 @@ def tile_picked_tokens_plain_twin_aboveaverage_store_plain_kernel(
                     stop=True,
                 )
                 result = keep.tile([P, HALF], F32, tag=f"result{h}{b}", name="result")
-                copy = nc.scalar.copy if b == 0 else nc.vector.tensor_copy
-                copy(result[:], acc[:, :HALF])
+                copies[b](result[:], acc[:, :HALF])
                 nc.sync.dma_start(out[rows, h * HALF : (h + 1) * HALF], result[:])
+
+        nc.vector.tensor_copy(grouped[1][:, :, 0], early[:, PACK, :])
+        nc.vector.tensor_copy(
+            grouped[0][:].rearrange("p (c i) t -> p c t i", i=4),
+            early[:, 0:PACK, :].rearrange("p t (c i) -> p c t i", i=4),
+        )
+        first_half = quantise(0)
+        nc.vector.tensor_copy(grouped[1][:, :, 1:last], late[:, 0 : last - 1, :].rearrange("p t c -> p c t"))
+        nc.vector.tensor_copy(grouped[1][:, :, last], late[:, last - 1, :])
+        second_half = quantise(1)
+        last_product(0, *first_half, (nc.scalar.copy, nc.scalar.copy))
+        last_product(1, *second_half, (nc.scalar.copy, nc.vector.tensor_copy))

@@ -88,9 +88,8 @@ def tile_picked_tokens_plain_twin_aboveaverage_store_plain_kernel(
         sa_tile = keep.tile([P, PACK], F32)
         nc.sync.dma_start(sa_tile[:], sa.rearrange("(p t) o -> p (t o)", t=PACK))
 
-        first_boards = [keep.tile([P, C], F32, name=f"first_board{i}") for i in range(2)]
-        for board in first_boards:
-            nc.vector.memset(board[:].bitcast(I32), 0)
+        first_boards = [keep.tile([P, C], F32, name="first_board")]
+        nc.vector.memset(first_boards[0][:].bitcast(I32), 0)
 
         words = [keep.tile([P, PACK, P], U32, name=f"dealt_words{i}", align_bytes=64) for i in range(2)]
         scales = [keep.tile([P, PACK, P], U8, name=f"dealt_scales{i}", align_bytes=64) for i in range(2)]
@@ -130,9 +129,10 @@ def tile_picked_tokens_plain_twin_aboveaverage_store_plain_kernel(
         deal(nc.scalar.copy, words[0], ww_raw[:], 1, PACK)
         gather(xs, xs_window, token_list, HALF, J)
         gather(xw, xw_window, token_list, XW1, J)
+        first_boards.append(keep.tile([P, C], F32, tag="token_words", name="first_board", align_bytes=64))
+        nc.vector.memset(first_boards[1][:].bitcast(I32), 0)
         product(0, 0, slice(HALF, J), 1, staged[0, 0], nc.vector.tensor_copy)
-        for t in range(1, PACK):
-            product(0, t, slice(0, J), 1 + t, staged[0, t], nc.vector.tensor_copy)
+        product(0, 1, slice(0, J), 2, staged[0, 1], nc.vector.tensor_copy)
         deal(nc.vector.tensor_copy, scales[1], w2s_raw[:])
         deal(nc.vector.tensor_copy, words[1], w2w_raw[:])
         second_boards = [
@@ -140,11 +140,14 @@ def tile_picked_tokens_plain_twin_aboveaverage_store_plain_kernel(
             for tag in ("early_rows", "second_scales")
         ]
         nc.vector.memset(second_boards[0][:].bitcast(I32), 0)
-        for t in range(PACK):
-            product(1, t, slice(0, J), (5 + t) % 8, staged[1, t], nc.vector.tensor_copy)
+        product(1, 0, slice(0, J), 3, staged[1, 0], nc.vector.tensor_copy)
         nc.vector.memset(second_boards[1][:].bitcast(I32), 0)
+        product(1, 1, slice(0, J), 4, staged[1, 1], nc.vector.tensor_copy)
+        for t in range(2, PACK):
+            for matrix in range(2):
+                product(matrix, t, slice(0, J), 3 + matrix, staged[matrix, t], nc.vector.tensor_copy)
 
-        vs_scale_window = keep.tile([P, S], U8, tag="token_words", align_bytes=64)
+        vs_scale_window = keep.tile([P, S], U8, tag="scale_window", align_bytes=64)
         nc.vector.memset(vs_scale_window[:].bitcast(I32), 0)
         load_scale_rows(vs_scale_window, vs_scales)
         vs_word_window = keep.tile([P, S], U32, tag="weight_words_raw", align_bytes=64)
@@ -200,39 +203,51 @@ def tile_picked_tokens_plain_twin_aboveaverage_store_plain_kernel(
             for tag in ("grouped", f"mean{last}")
         ]
 
-        def quantise(h):
-            codes = keep.tile([P, HALF], U32, tag=f"codes{h}", name="codes", align_bytes=64)
-            code_scales = keep.tile([P, HALF], U8, tag=f"code_scales{h}", name="code_scales", align_bytes=64)
-            nc.vector.quantize_mx(
-                out=codes[:].bitcast(FP8X4), scales=code_scales[:], in_=grouped[h][:].rearrange("p c t -> p (c t)")
-            )
-            return codes, code_scales
+        codes = keep.tile([P, O], U32, align_bytes=64)
+        code_scales = keep.tile([P, O], U8, align_bytes=64)
+        results = keep.tile([P, N // P, O], F32)
 
-        def last_product(h, codes, code_scales, copies):
-            for b in range(N // P):
-                rows = slice(b * P, (b + 1) * P)
-                acc = psum.tile([P, J], F32, tag=f"bank{2 * h + b + 1}", name="acc")
-                nc.tensor.matmul_mx(
-                    out=acc[:, :HALF],
-                    lhsT=vw[:, rows].bitcast(FP8X4),
-                    lhsT_scale=vsc[:, rows],
-                    rhs=codes[:].bitcast(FP8X4),
-                    rhs_scale=code_scales[:],
-                    start=True,
-                    stop=True,
-                )
-                result = keep.tile([P, HALF], F32, tag=f"result{h}{b}", name="result")
-                copies[b](result[:], acc[:, :HALF])
-                nc.sync.dma_start(out[rows, h * HALF : (h + 1) * HALF], result[:])
+        def quantise(first, last_col):
+            h, base = divmod(first, HALF)
+            nc.vector.quantize_mx(
+                out=codes[:, first:last_col].bitcast(FP8X4),
+                scales=code_scales[:, first:last_col],
+                in_=grouped[h][:, base : base + last_col - first, :].rearrange("p c t -> p (c t)"),
+            )
+
+        def last_product(b, first, last_col, bank, copy):
+            rows = slice(b * P, (b + 1) * P)
+            acc = psum.tile([P, J], F32, tag=f"bank{bank}", name="acc")
+            nc.tensor.matmul_mx(
+                out=acc[:, : last_col - first],
+                lhsT=vw[:, rows].bitcast(FP8X4),
+                lhsT_scale=vsc[:, rows],
+                rhs=codes[:, first:last_col].bitcast(FP8X4),
+                rhs_scale=code_scales[:, first:last_col],
+                start=True,
+                stop=True,
+            )
+            copy(results[:, b, first:last_col], acc[:, : last_col - first])
+
+        def store(first, last_col):
+            rows = out.rearrange("(b p) o -> p b o", p=P)
+            nc.sync.dma_start(rows[:, :, first:last_col], results[:, :, first:last_col])
 
         nc.vector.tensor_copy(grouped[1][:, :, 0], early[:, PACK, :])
         nc.vector.tensor_copy(
             grouped[0][:].rearrange("p (c i) t -> p c t i", i=4),
             early[:, 0:PACK, :].rearrange("p t (c i) -> p c t i", i=4),
         )
-        first_half = quantise(0)
+        quantise(0, HALF)
         nc.vector.tensor_copy(grouped[1][:, :, 1:last], late[:, 0 : last - 1, :].rearrange("p t c -> p c t"))
-        nc.vector.tensor_copy(grouped[1][:, :, last], late[:, last - 1, :])
-        second_half = quantise(1)
-        last_product(0, *first_half, (nc.scalar.copy, nc.scalar.copy))
-        last_product(1, *second_half, (nc.scalar.copy, nc.vector.tensor_copy))
+        for first in range(0, HALF, P):
+            nc.vector.tensor_copy(grouped[1][:, first : first + P, last], late[:, last - 1, first : first + P])
+        for first in range(HALF, O, P):
+            quantise(first, first + P)
+        for b in range(N // P):
+            last_product(b, 0, HALF, b, nc.scalar.copy)
+        store(0, HALF)
+        for first in range(HALF, O, P):
+            last_product(0, first, first + P, 2 * first // P - 2, nc.scalar.copy)
+            last_product(1, first, first + P, 2 * first // P - 1, nc.vector.tensor_copy)
+            store(first, first + P)

@@ -21,7 +21,9 @@ PACK = 4
 QUAD = 32
 HALF = 256
 LIST_ROWS = 16
-XW1 = HALF - 32
+RUN = 4
+LAST = PACK - 1
+FIRST, SECOND = 0, 1
 
 
 def tile_picked_tokens_plain_twin_aboveaverage_store_plain_kernel(
@@ -39,128 +41,137 @@ def tile_picked_tokens_plain_twin_aboveaverage_store_plain_kernel(
             nc.sync.dma_start(tile[:], source)
             return tile
 
-        def entries(tile, first, count):
-            return tile[:, first // LIST_ROWS : (first + count) // LIST_ROWS]
+        def entries(list_tile, first, end):
+            return list_tile[:, first // LIST_ROWS : end // LIST_ROWS]
 
-        def load_scale_rows(plane, source):
+        def clear(tile):
+            nc.vector.memset(tile[:].bitcast(I32), 0)
+
+        def load_scale_rows(tile, source):
             for q in range(P // QUAD):
                 nc.sync.dma_start(
-                    plane[QUAD * q : QUAD * q + PACK, :].bitcast(I32),
+                    tile[QUAD * q : QUAD * q + PACK, :].bitcast(I32),
                     source[0, PACK * q : PACK * (q + 1), :].bitcast(I32),
-                )
-
-        def spread_scale_rows(plane, rows):
-            for q in range(P // QUAD):
-                nc.vector.tensor_copy(
-                    plane[QUAD * q : QUAD * q + PACK, :].bitcast(I32), rows[0:PACK, q, :].bitcast(I32)
                 )
 
         def load_words(tile, source):
             nc.sync.dma_start(tile[:].bitcast(I32), source[0].rearrange("p n t -> p (n t)").bitcast(I32))
 
-        def deal(copy, dealt, raw, first=0, last=PACK):
-            copy(
-                dealt[:, first:last, :].rearrange("p t m -> p m t"),
-                raw.rearrange("p (m t) -> p m t", t=PACK)[:, :, first:last],
-            )
+        def deal(copy, dealt, raw, first, end):
+            copy(dealt.rearrange("p t m -> p m t"), raw[:].rearrange("p (m t) -> p m t", t=PACK)[:, :, first:end])
 
-        xs_window = keep.tile([P, T], U8, tag="scale_window", align_bytes=64)
-        nc.vector.memset(xs_window[:].bitcast(I32), 0)
+        def gather(dst, window, list_tile, first, end):
+            nc.vector.tensor_copy(dst, window[:].indirect(entries(list_tile, first, end)))
+
+        token_scale_window = keep.tile([P, T], U8, tag="scale_window", align_bytes=64)
+        clear(token_scale_window)
         token_list = load_list(offs, "token_list")
-        ws_rows = keep.tile([PACK, P // QUAD, R], U8, tag="early_rows", align_bytes=64)
-        nc.sync.dma_start(
-            ws_rows[:].bitcast(I32), w_scales[0].rearrange("(q i) c -> i q c", i=PACK).bitcast(I32)
-        )
-        xw_window = keep.tile([P, T], U16, tag="token_words", align_bytes=64)
-        nc.sync.dma_start(xw_window[:].bitcast(I32), xt_words[0].bitcast(I32))
-        load_scale_rows(xs_window, xt_scales)
-        ww_raw = keep.tile([P, R], U32, tag="weight_words_raw", align_bytes=64)
-        load_words(ww_raw, w_words)
-        ws_raw = keep.tile([P, R], U8, align_bytes=64)
-        nc.vector.memset(ws_raw[:].bitcast(I32), 0)
-        w2s_raw = keep.tile([P, R], U8, tag="second_scales", align_bytes=64)
-        nc.vector.memset(w2s_raw[:].bitcast(I32), 0)
-        first_list = load_list(offs2, "first_board_list")
-        load_scale_rows(w2s_raw, w2_scales)
-        board_lists = [first_list, load_list(offs3, "second_board_list")]
+        w_scale_rows = keep.tile([PACK, P // QUAD, R], U8, tag="early_rows", align_bytes=64)
+        nc.sync.dma_start(w_scale_rows[:].bitcast(I32), w_scales[0].rearrange("(q i) c -> i q c", i=PACK).bitcast(I32))
+        token_word_window = keep.tile([P, T], U16, tag="token_word_window", align_bytes=64)
+        nc.sync.dma_start(token_word_window[:].bitcast(I32), xt_words[0].bitcast(I32))
+        load_scale_rows(token_scale_window, xt_scales)
+        w_words_raw = keep.tile([P, R], U32, tag="w_words_raw", align_bytes=64)
+        load_words(w_words_raw, w_words)
+        w_scales_raw = keep.tile([P, R], U8, tag="w_scales_raw", align_bytes=64)
+        clear(w_scales_raw)
+        w2_scales_raw = keep.tile([P, R], U8, tag="w2_scales_raw", align_bytes=64)
+        clear(w2_scales_raw)
+        first_list = load_list(offs2, "first_list")
+        load_scale_rows(w2_scales_raw, w2_scales)
+        second_list = load_list(offs3, "second_list")
         place_list = load_list(offs4, "place_list")
         store_list = load_list(offs5, "store_list")
         sa_tile = keep.tile([P, PACK], F32)
         nc.sync.dma_start(sa_tile[:], sa.rearrange("(p t) o -> p (t o)", t=PACK))
 
         first_boards = [keep.tile([P, C], F32, name="first_board")]
-        nc.vector.memset(first_boards[0][:].bitcast(I32), 0)
+        clear(first_boards[0])
 
-        words = [keep.tile([P, PACK, P], U32, name=f"dealt_words{i}", align_bytes=64) for i in range(2)]
-        scales = [keep.tile([P, PACK, P], U8, name=f"dealt_scales{i}", align_bytes=64) for i in range(2)]
-        xw = keep.tile([P, J], U16, align_bytes=64)
-        xs = keep.tile([P, J], U8, align_bytes=64)
+        words = [keep.tile([P, PACK, P], U32, name=f"dealt_words{m}", align_bytes=64) for m in (FIRST, SECOND)]
+        scales = {}
+        token_words = []
+        token_scales = keep.tile([P, J], U8, align_bytes=64)
+        staged = {
+            (m, t): keep.tile([P, J], F32, tag=f"staged{m}{t}", name="staged", align_bytes=64)
+            for t in range(PACK)
+            for m in (FIRST, SECOND)
+        }
 
-        def gather(dst, window, offsets, first, last):
-            nc.vector.tensor_copy(dst[:, first:last], window[:].indirect(entries(offsets, first, last - first)))
-
-        def product(matrix, t, cols, bank, staged, copy):
-            width = cols.stop - cols.start
+        def product(m, t, halves, bank, copy):
             acc = psum.tile([P, J], F32, tag=f"bank{bank}", name="acc")
-            nc.tensor.matmul_mx(
-                out=acc[:, :width],
-                lhsT=words[matrix][:, t, :].bitcast(FP8X4),
-                lhsT_scale=scales[matrix][:, t, :],
-                rhs=xw[:, cols].bitcast(FP4X4),
-                rhs_scale=xs[:, cols],
-                start=True,
-                stop=True,
+            for h in halves:
+                cols = slice(h * HALF, (h + 1) * HALF)
+                nc.tensor.matmul_mx(
+                    out=acc[:, cols],
+                    lhsT=words[m][:, t, :].bitcast(FP8X4),
+                    lhsT_scale=scales[m, t],
+                    rhs=token_words[h][:].bitcast(FP4X4),
+                    rhs_scale=token_scales[:, cols],
+                    start=True,
+                    stop=True,
+                )
+            cols = slice(halves[0] * HALF, (halves[-1] + 1) * HALF)
+            copy(staged[m, t][:, cols], acc[:, cols])
+
+        for q in range(P // QUAD):
+            nc.vector.tensor_copy(
+                w_scales_raw[QUAD * q : QUAD * q + PACK, :].bitcast(I32), w_scale_rows[:, q, :].bitcast(I32)
             )
-            copy(staged[:, cols], acc[:, :width])
+        w2_words_raw = keep.tile([P, R], U32, tag="early_rows", align_bytes=64)
+        load_words(w2_words_raw, w2_words)
+        lead_scales = keep.tile([P, 1, P], U8, align_bytes=64)
+        deal(nc.vector.tensor_copy, lead_scales[:], w_scales_raw, 0, 1)
+        scales[FIRST, 0] = lead_scales[:, 0, :]
+        deal(nc.scalar.copy, words[FIRST][:, 0:1, :], w_words_raw, 0, 1)
+        token_words.append(keep.tile([P, HALF], U16, name="token_words", align_bytes=64))
+        gather(token_words[0][:], token_word_window, token_list, 0, HALF)
+        gather(token_scales[:, 0:HALF], token_scale_window, token_list, 0, HALF)
+        product(FIRST, 0, [0], 0, nc.scalar.copy)
 
-        staged = {}
+        deal(nc.scalar.copy, words[FIRST][:, 1:, :], w_words_raw, 1, PACK)
+        gather(token_scales[:, HALF:J], token_scale_window, token_list, HALF, J)
+        other_scales = keep.tile([P, LAST, P], U8, tag="scale_window", align_bytes=64)
+        deal(nc.vector.tensor_copy, other_scales[:], w_scales_raw, 1, PACK)
+        for t in range(1, PACK):
+            scales[FIRST, t] = other_scales[:, t - 1, :]
+        token_words.append(keep.tile([P, HALF], U16, tag="w_scales_raw", name="token_words", align_bytes=64))
+        gather(token_words[1][:], token_word_window, token_list, HALF, J)
+        first_boards.append(keep.tile([P, C], F32, tag="token_word_window", name="first_board", align_bytes=64))
+        clear(first_boards[1])
+        product(FIRST, 0, [1], 1, nc.vector.tensor_copy)
+        product(FIRST, 1, [0, 1], 2, nc.vector.tensor_copy)
+
+        w2_dealt_scales = keep.tile([P, PACK, P], U8, align_bytes=64)
+        deal(nc.vector.tensor_copy, w2_dealt_scales[:], w2_scales_raw, 0, PACK)
         for t in range(PACK):
-            for matrix in range(2):
-                staged[matrix, t] = keep.tile([P, J], F32, tag=f"staged{matrix}{t}", name="staged", align_bytes=64)
-
-        spread_scale_rows(ws_raw, ws_rows)
-        w2w_raw = keep.tile([P, R], U32, tag="early_rows", align_bytes=64)
-        load_words(w2w_raw, w2_words)
-        deal(nc.vector.tensor_copy, scales[0], ws_raw[:])
-        deal(nc.scalar.copy, words[0], ww_raw[:], 0, 1)
-        gather(xw, xw_window, token_list, 0, HALF)
-        gather(xs, xs_window, token_list, 0, HALF)
-        product(0, 0, slice(0, HALF), 0, staged[0, 0], nc.scalar.copy)
-        deal(nc.scalar.copy, words[0], ww_raw[:], 1, PACK)
-        gather(xs, xs_window, token_list, HALF, J)
-        gather(xw, xw_window, token_list, XW1, J)
-        first_boards.append(keep.tile([P, C], F32, tag="token_words", name="first_board", align_bytes=64))
-        nc.vector.memset(first_boards[1][:].bitcast(I32), 0)
-        product(0, 0, slice(HALF, J), 1, staged[0, 0], nc.vector.tensor_copy)
-        product(0, 1, slice(0, J), 2, staged[0, 1], nc.vector.tensor_copy)
-        deal(nc.vector.tensor_copy, scales[1], w2s_raw[:])
-        deal(nc.vector.tensor_copy, words[1], w2w_raw[:])
+            scales[SECOND, t] = w2_dealt_scales[:, t, :]
+        deal(nc.vector.tensor_copy, words[SECOND][:], w2_words_raw, 0, PACK)
         second_boards = [
             keep.tile([P, C], F32, tag=tag, name="second_board", align_bytes=64)
-            for tag in ("early_rows", "second_scales")
+            for tag in ("early_rows", "w2_scales_raw")
         ]
-        nc.vector.memset(second_boards[0][:].bitcast(I32), 0)
-        product(1, 0, slice(0, J), 3, staged[1, 0], nc.vector.tensor_copy)
-        nc.vector.memset(second_boards[1][:].bitcast(I32), 0)
-        product(1, 1, slice(0, J), 4, staged[1, 1], nc.vector.tensor_copy)
+        for t in range(2):
+            clear(second_boards[t])
+            product(SECOND, t, [0, 1], 3 + t, nc.vector.tensor_copy)
         for t in range(2, PACK):
-            for matrix in range(2):
-                product(matrix, t, slice(0, J), 3 + matrix, staged[matrix, t], nc.vector.tensor_copy)
+            for m in (FIRST, SECOND):
+                product(m, t, [0, 1], 3 + m, nc.vector.tensor_copy)
 
-        vs_scale_window = keep.tile([P, S], U8, tag="scale_window", align_bytes=64)
-        nc.vector.memset(vs_scale_window[:].bitcast(I32), 0)
-        load_scale_rows(vs_scale_window, vs_scales)
-        vs_word_window = keep.tile([P, S], U32, tag="weight_words_raw", align_bytes=64)
-        load_words(vs_word_window, vs_words)
-        vw = keep.tile([P, N], U32, align_bytes=64)
-        vsc = keep.tile([P, N], U8, align_bytes=64)
-        nc.vector.tensor_copy(vw[:], vs_word_window[:].indirect(store_list[:]))
-        nc.vector.tensor_copy(vsc[:], vs_scale_window[:].indirect(store_list[:]))
+        store_scale_window = keep.tile([P, S], U8, tag="scale_window", align_bytes=64)
+        clear(store_scale_window)
+        load_scale_rows(store_scale_window, vs_scales)
+        store_word_window = keep.tile([P, S], U32, tag="w_words_raw", align_bytes=64)
+        load_words(store_word_window, vs_words)
+        store_words = keep.tile([P, N], U32, align_bytes=64)
+        store_scales = keep.tile([P, N], U8, align_bytes=64)
+        gather(store_words[:], store_word_window, store_list, 0, N)
+        gather(store_scales[:], store_scale_window, store_list, 0, N)
 
-        def scatter(board, offsets, values, first, last):
-            nc.scalar.activation(board[:].indirect(entries(offsets, first, last - first)), values[:, first:last], COPY)
+        def scatter(board, list_tile, values, first, end):
+            nc.scalar.activation(board[:].indirect(entries(list_tile, first, end)), values[:, first:end], COPY)
 
-        def compare(t):
+        def above_mean(t):
             larger = keep.tile([P, C], F32, tag="larger", name="larger", align_bytes=64)
             total = keep.tile([P, 1], F32, tag=f"total{t}", name="total")
             nc.vector.scalar_tensor_tensor(
@@ -168,86 +179,84 @@ def tile_picked_tokens_plain_twin_aboveaverage_store_plain_kernel(
             )
             mean = keep.tile([P, 1], F32, tag=f"mean{t}", name="mean", align_bytes=64)
             nc.vector.tensor_scalar(mean[:], total[:], 1.0 / C, None, ALU.mult)
-            excess = keep.tile([P, C], F32, tag=f"excess{t}", name="excess")
-            nc.vector.tensor_scalar(excess[:], larger[:], mean[:], 0.0, ALU.subtract, ALU.max)
-            return excess
+            g1_rows = keep.tile([P, C], F32, tag=f"g1_rows{t}", name="g1_rows")
+            nc.vector.tensor_scalar(g1_rows[:], larger[:], mean[:], 0.0, ALU.subtract, ALU.max)
+            return g1_rows
 
-        scatter(first_boards[0], board_lists[0], staged[0, 0], 0, HALF)
-        scatter(first_boards[0], board_lists[0], staged[0, 0], HALF, J)
-        scatter(first_boards[1], board_lists[0], staged[0, 1], 0, J)
-        above = []
+        scatter(first_boards[0], first_list, staged[FIRST, 0], 0, HALF)
+        scatter(first_boards[0], first_list, staged[FIRST, 0], HALF, J)
+        scatter(first_boards[1], first_list, staged[FIRST, 1], 0, J)
+        g1 = []
         for t in range(PACK):
-            if t >= 2:
-                scatter(first_boards[t % 2], board_lists[0], staged[0, t], 0, J)
-            scatter(second_boards[t % 2], board_lists[1], staged[1, t], 0, J)
-            above.append(compare(t))
+            if t >= len(first_boards):
+                scatter(first_boards[t % 2], first_list, staged[FIRST, t], 0, J)
+            scatter(second_boards[t % 2], second_list, staged[SECOND, t], 0, J)
+            g1.append(above_mean(t))
 
-        last = PACK - 1
-        early = keep.tile([P, PACK + 1, HALF], BF16, tag=f"staged1{last}", align_bytes=64)
-        late = keep.tile([P, last, HALF], BF16, tag="larger", align_bytes=64)
+        hid_early = keep.tile([P, PACK + 1, HALF], BF16, tag=f"staged{SECOND}{LAST}", align_bytes=64)
+        hid_late = keep.tile([P, LAST, HALF], BF16, tag="larger", align_bytes=64)
 
         def fetch(dst, t, h):
             nc.scalar.activation(
-                dst, above[t][:].indirect(entries(place_list, h * HALF, HALF)), COPY, scale=sa_tile[:, t : t + 1]
+                dst, g1[t][:].indirect(entries(place_list, h * HALF, (h + 1) * HALF)), COPY, scale=sa_tile[:, t : t + 1]
             )
 
-        for t in range(last):
-            fetch(early[:, t, :], t, 0)
-        fetch(early[:, PACK, :], 0, 1)
-        fetch(early[:, last, :], last, 0)
+        for t in range(LAST):
+            fetch(hid_early[:, t, :], t, 0)
+        fetch(hid_early[:, PACK, :], 0, 1)
+        fetch(hid_early[:, LAST, :], LAST, 0)
         for t in range(1, PACK):
-            fetch(late[:, t - 1, :], t, 1)
+            fetch(hid_late[:, t - 1, :], t, 1)
 
         grouped = [
             keep.tile([P, HALF, PACK], BF16, tag=tag, name="grouped", align_bytes=64)
-            for tag in ("grouped", f"mean{last}")
+            for tag in ("grouped", f"mean{LAST}")
         ]
-
         codes = keep.tile([P, O], U32, align_bytes=64)
         code_scales = keep.tile([P, O], U8, align_bytes=64)
-        results = keep.tile([P, N // P, O], F32)
+        results = [keep.tile([P, O], F32, name=f"result{b}") for b in range(N // P)]
 
-        def quantise(first, last_col):
+        def quantise(first, end):
             h, base = divmod(first, HALF)
             nc.vector.quantize_mx(
-                out=codes[:, first:last_col].bitcast(FP8X4),
-                scales=code_scales[:, first:last_col],
-                in_=grouped[h][:, base : base + last_col - first, :].rearrange("p c t -> p (c t)"),
+                out=codes[:, first:end].bitcast(FP8X4),
+                scales=code_scales[:, first:end],
+                in_=grouped[h][:, base : base + end - first, :].rearrange("p c t -> p (c t)"),
             )
 
-        def last_product(b, first, last_col, bank, copy):
+        def last_product(b, first, end, bank, copy):
             rows = slice(b * P, (b + 1) * P)
             acc = psum.tile([P, J], F32, tag=f"bank{bank}", name="acc")
             nc.tensor.matmul_mx(
-                out=acc[:, : last_col - first],
-                lhsT=vw[:, rows].bitcast(FP8X4),
-                lhsT_scale=vsc[:, rows],
-                rhs=codes[:, first:last_col].bitcast(FP8X4),
-                rhs_scale=code_scales[:, first:last_col],
+                out=acc[:, : end - first],
+                lhsT=store_words[:, rows].bitcast(FP8X4),
+                lhsT_scale=store_scales[:, rows],
+                rhs=codes[:, first:end].bitcast(FP8X4),
+                rhs_scale=code_scales[:, first:end],
                 start=True,
                 stop=True,
             )
-            copy(results[:, b, first:last_col], acc[:, : last_col - first])
+            copy(results[b][:, first:end], acc[:, : end - first])
 
-        def store(first, last_col):
-            rows = out.rearrange("(b p) o -> p b o", p=P)
-            nc.sync.dma_start(rows[:, :, first:last_col], results[:, :, first:last_col])
+        def store(b, first, end):
+            nc.sync.dma_start(out[b * P : (b + 1) * P, first:end], results[b][:, first:end])
 
-        nc.vector.tensor_copy(grouped[1][:, :, 0], early[:, PACK, :])
+        nc.vector.tensor_copy(grouped[1][:, :, 0], hid_early[:, PACK, :])
         nc.vector.tensor_copy(
-            grouped[0][:].rearrange("p (c i) t -> p c t i", i=4),
-            early[:, 0:PACK, :].rearrange("p t (c i) -> p c t i", i=4),
+            grouped[0][:].rearrange("p (c i) t -> p c t i", i=RUN),
+            hid_early[:, 0:PACK, :].rearrange("p t (c i) -> p c t i", i=RUN),
         )
         quantise(0, HALF)
-        nc.vector.tensor_copy(grouped[1][:, :, 1:last], late[:, 0 : last - 1, :].rearrange("p t c -> p c t"))
+        nc.vector.tensor_copy(grouped[1][:, :, 1:LAST], hid_late[:, 0 : LAST - 1, :].rearrange("p t c -> p c t"))
         for first in range(0, HALF, P):
-            nc.vector.tensor_copy(grouped[1][:, first : first + P, last], late[:, last - 1, first : first + P])
+            nc.vector.tensor_copy(grouped[1][:, first : first + P, LAST], hid_late[:, LAST - 1, first : first + P])
         for first in range(HALF, O, P):
             quantise(first, first + P)
         for b in range(N // P):
             last_product(b, 0, HALF, b, nc.scalar.copy)
-        store(0, HALF)
-        for first in range(HALF, O, P):
-            last_product(0, first, first + P, 2 * first // P - 2, nc.scalar.copy)
-            last_product(1, first, first + P, 2 * first // P - 1, nc.vector.tensor_copy)
-            store(first, first + P)
+            store(b, 0, HALF)
+        for piece, first in enumerate(range(HALF, O, P)):
+            last_product(0, first, first + P, 2 + 2 * piece, nc.scalar.copy)
+            last_product(1, first, first + P, 3 + 2 * piece, nc.vector.tensor_copy)
+        for b in range(N // P):
+            store(b, HALF, O)

from contextlib import ExitStack

import concourse.mybir as mybir

K, J, R, T, C, O, N, S = 512, 512, 512, 2048, 1024, 512, 256, 1024
FLOPS = 2 * (2 * K * R * J + R * N * O)

F32 = mybir.dt.float32
BF16 = mybir.dt.bfloat16
I32 = mybir.dt.int32
U32 = mybir.dt.uint32
U16 = mybir.dt.uint16
U8 = mybir.dt.uint8
FP8X4 = mybir.dt.float8_e4m3fn_x4
FP4X4 = mybir.dt.float4_e2m1fn_x4
ALU = mybir.AluOpType
COPY = mybir.ActivationFunctionType.Copy

P = 128
PACK = 4
QUAD = 32
HALF = 256
LIST_ROWS = 16
RUN = 4
LAST = PACK - 1
FIRST, SECOND = 0, 1


def tile_picked_tokens_plain_twin_aboveaverage_store_plain_kernel(
    tc, xt_words, xt_scales, w_words, w_scales, w2_words, w2_scales, sa, vs_words, vs_scales,
    offs, offs2, offs3, offs4, offs5, out,
):
    nc = tc.nc
    with ExitStack() as ctx:
        lists = ctx.enter_context(tc.tile_pool(name="lists", bufs=1))
        keep = ctx.enter_context(tc.tile_pool(name="keep", bufs=1))
        psum = ctx.enter_context(tc.psum_pool(name="psum", bufs=1))

        def load_list(source, name):
            tile = lists.tile(list(source.shape), U16, name=name)
            nc.sync.dma_start(tile[:], source)
            return tile

        def entries(list_tile, first, end):
            return list_tile[:, first // LIST_ROWS : end // LIST_ROWS]

        def clear(tile):
            nc.vector.memset(tile[:].bitcast(I32), 0)

        def load_scale_rows(tile, source):
            for q in range(P // QUAD):
                nc.sync.dma_start(
                    tile[QUAD * q : QUAD * q + PACK, :].bitcast(I32),
                    source[0, PACK * q : PACK * (q + 1), :].bitcast(I32),
                )

        def load_words(tile, source):
            nc.sync.dma_start(tile[:].bitcast(I32), source[0].rearrange("p n t -> p (n t)").bitcast(I32))

        def deal(copy, dealt, raw, first, end):
            copy(dealt.rearrange("p t m -> p m t"), raw[:].rearrange("p (m t) -> p m t", t=PACK)[:, :, first:end])

        def gather(dst, window, list_tile, first, end):
            nc.vector.tensor_copy(dst, window[:].indirect(entries(list_tile, first, end)))

        token_scale_window = keep.tile([P, T], U8, tag="scale_window", align_bytes=64)
        clear(token_scale_window)
        token_list = load_list(offs, "token_list")
        w_scale_rows = keep.tile([PACK, P // QUAD, R], U8, tag="early_rows", align_bytes=64)
        nc.sync.dma_start(w_scale_rows[:].bitcast(I32), w_scales[0].rearrange("(q i) c -> i q c", i=PACK).bitcast(I32))
        token_word_window = keep.tile([P, T], U16, tag="token_word_window", align_bytes=64)
        nc.sync.dma_start(token_word_window[:].bitcast(I32), xt_words[0].bitcast(I32))
        load_scale_rows(token_scale_window, xt_scales)
        w_words_raw = keep.tile([P, R], U32, tag="w_words_raw", align_bytes=64)
        load_words(w_words_raw, w_words)
        w_scales_raw = keep.tile([P, R], U8, tag="w_scales_raw", align_bytes=64)
        clear(w_scales_raw)
        w2_scales_raw = keep.tile([P, R], U8, tag="w2_scales_raw", align_bytes=64)
        clear(w2_scales_raw)
        first_list = load_list(offs2, "first_list")
        load_scale_rows(w2_scales_raw, w2_scales)
        second_list = load_list(offs3, "second_list")
        place_list = load_list(offs4, "place_list")
        store_list = load_list(offs5, "store_list")
        sa_tile = keep.tile([P, PACK], F32)
        nc.sync.dma_start(sa_tile[:], sa.rearrange("(p t) o -> p (t o)", t=PACK))

        first_boards = [keep.tile([P, C], F32, name="first_board")]
        clear(first_boards[0])

        words = [keep.tile([P, PACK, P], U32, name=f"dealt_words{m}", align_bytes=64) for m in (FIRST, SECOND)]
        scales = {}
        token_words = []
        token_scales = keep.tile([P, J], U8, align_bytes=64)
        staged = {
            (m, t): keep.tile([P, J], F32, tag=f"staged{m}{t}", name="staged", align_bytes=64)
            for t in range(PACK)
            for m in (FIRST, SECOND)
        }

        def product(m, t, halves, bank, copy):
            acc = psum.tile([P, J], F32, tag=f"bank{bank}", name="acc")
            for h in halves:
                cols = slice(h * HALF, (h + 1) * HALF)
                nc.tensor.matmul_mx(
                    out=acc[:, cols],
                    lhsT=words[m][:, t, :].bitcast(FP8X4),
                    lhsT_scale=scales[m, t],
                    rhs=token_words[h][:].bitcast(FP4X4),
                    rhs_scale=token_scales[:, cols],
                    start=True,
                    stop=True,
                )
            cols = slice(halves[0] * HALF, (halves[-1] + 1) * HALF)
            copy(staged[m, t][:, cols], acc[:, cols])

        for q in range(P // QUAD):
            nc.vector.tensor_copy(
                w_scales_raw[QUAD * q : QUAD * q + PACK, :].bitcast(I32), w_scale_rows[:, q, :].bitcast(I32)
            )
        w2_words_raw = keep.tile([P, R], U32, tag="early_rows", align_bytes=64)
        load_words(w2_words_raw, w2_words)
        lead_scales = keep.tile([P, 1, P], U8, align_bytes=64)
        deal(nc.vector.tensor_copy, lead_scales[:], w_scales_raw, 0, 1)
        scales[FIRST, 0] = lead_scales[:, 0, :]
        deal(nc.scalar.copy, words[FIRST][:, 0:1, :], w_words_raw, 0, 1)
        token_words.append(keep.tile([P, HALF], U16, name="token_words", align_bytes=64))
        gather(token_words[0][:], token_word_window, token_list, 0, HALF)
        gather(token_scales[:, 0:HALF], token_scale_window, token_list, 0, HALF)
        product(FIRST, 0, [0], 0, nc.scalar.copy)

        deal(nc.scalar.copy, words[FIRST][:, 1:, :], w_words_raw, 1, PACK)
        gather(token_scales[:, HALF:J], token_scale_window, token_list, HALF, J)
        other_scales = keep.tile([P, LAST, P], U8, tag="scale_window", align_bytes=64)
        deal(nc.vector.tensor_copy, other_scales[:], w_scales_raw, 1, PACK)
        for t in range(1, PACK):
            scales[FIRST, t] = other_scales[:, t - 1, :]
        token_words.append(keep.tile([P, HALF], U16, tag="w_scales_raw", name="token_words", align_bytes=64))
        gather(token_words[1][:], token_word_window, token_list, HALF, J)
        first_boards.append(keep.tile([P, C], F32, tag="token_word_window", name="first_board", align_bytes=64))
        clear(first_boards[1])
        product(FIRST, 0, [1], 1, nc.vector.tensor_copy)
        product(FIRST, 1, [0, 1], 2, nc.vector.tensor_copy)

        w2_dealt_scales = keep.tile([P, PACK, P], U8, align_bytes=64)
        deal(nc.vector.tensor_copy, w2_dealt_scales[:], w2_scales_raw, 0, PACK)
        for t in range(PACK):
            scales[SECOND, t] = w2_dealt_scales[:, t, :]
        deal(nc.vector.tensor_copy, words[SECOND][:], w2_words_raw, 0, PACK)
        second_boards = [
            keep.tile([P, C], F32, tag=tag, name="second_board", align_bytes=64)
            for tag in ("early_rows", "w2_scales_raw")
        ]
        for t in range(2):
            clear(second_boards[t])
            product(SECOND, t, [0, 1], 3 + t, nc.vector.tensor_copy)
        for t in range(2, PACK):
            for m in (FIRST, SECOND):
                product(m, t, [0, 1], 3 + m, nc.vector.tensor_copy)

        store_scale_window = keep.tile([P, S], U8, tag="scale_window", align_bytes=64)
        clear(store_scale_window)
        load_scale_rows(store_scale_window, vs_scales)
        store_word_window = keep.tile([P, S], U32, tag="w_words_raw", align_bytes=64)
        load_words(store_word_window, vs_words)
        store_words = keep.tile([P, N], U32, align_bytes=64)
        store_scales = keep.tile([P, N], U8, align_bytes=64)
        gather(store_words[:], store_word_window, store_list, 0, N)
        gather(store_scales[:], store_scale_window, store_list, 0, N)

        def scatter(board, list_tile, values, first, end):
            nc.scalar.activation(board[:].indirect(entries(list_tile, first, end)), values[:, first:end], COPY)

        def above_mean(t):
            larger = keep.tile([P, C], F32, tag="larger", name="larger", align_bytes=64)
            total = keep.tile([P, 1], F32, tag=f"total{t}", name="total")
            nc.vector.scalar_tensor_tensor(
                larger[:], first_boards[t % 2][:], 1.0, second_boards[t % 2][:], ALU.mult, ALU.max, accum_out=total[:]
            )
            mean = keep.tile([P, 1], F32, tag=f"mean{t}", name="mean", align_bytes=64)
            nc.vector.tensor_scalar(mean[:], total[:], 1.0 / C, None, ALU.mult)
            g1_rows = keep.tile([P, C], F32, tag=f"g1_rows{t}", name="g1_rows")
            nc.vector.tensor_scalar(g1_rows[:], larger[:], mean[:], 0.0, ALU.subtract, ALU.max)
            return g1_rows

        scatter(first_boards[0], first_list, staged[FIRST, 0], 0, HALF)
        scatter(first_boards[0], first_list, staged[FIRST, 0], HALF, J)
        scatter(first_boards[1], first_list, staged[FIRST, 1], 0, J)
        g1 = []
        for t in range(PACK):
            if t >= len(first_boards):
                scatter(first_boards[t % 2], first_list, staged[FIRST, t], 0, J)
            scatter(second_boards[t % 2], second_list, staged[SECOND, t], 0, J)
            g1.append(above_mean(t))

        hid_early = keep.tile([P, PACK + 1, HALF], BF16, tag=f"staged{SECOND}{LAST}", align_bytes=64)
        hid_late = keep.tile([P, LAST, HALF], BF16, tag="larger", align_bytes=64)

        def fetch(dst, t, h):
            nc.scalar.activation(
                dst, g1[t][:].indirect(entries(place_list, h * HALF, (h + 1) * HALF)), COPY, scale=sa_tile[:, t : t + 1]
            )

        for t in range(LAST):
            fetch(hid_early[:, t, :], t, 0)
        fetch(hid_early[:, PACK, :], 0, 1)
        fetch(hid_early[:, LAST, :], LAST, 0)
        for t in range(1, PACK):
            fetch(hid_late[:, t - 1, :], t, 1)

        grouped = [
            keep.tile([P, HALF, PACK], BF16, tag=tag, name="grouped", align_bytes=64)
            for tag in ("grouped", f"mean{LAST}")
        ]
        codes = keep.tile([P, O], U32, align_bytes=64)
        code_scales = keep.tile([P, O], U8, align_bytes=64)
        results = [keep.tile([P, O], F32, name=f"result{b}") for b in range(N // P)]

        def quantise(first, end):
            h, base = divmod(first, HALF)
            nc.vector.quantize_mx(
                out=codes[:, first:end].bitcast(FP8X4),
                scales=code_scales[:, first:end],
                in_=grouped[h][:, base : base + end - first, :].rearrange("p c t -> p (c t)"),
            )

        def last_product(b, first, end, bank, copy):
            rows = slice(b * P, (b + 1) * P)
            acc = psum.tile([P, J], F32, tag=f"bank{bank}", name="acc")
            nc.tensor.matmul_mx(
                out=acc[:, : end - first],
                lhsT=store_words[:, rows].bitcast(FP8X4),
                lhsT_scale=store_scales[:, rows],
                rhs=codes[:, first:end].bitcast(FP8X4),
                rhs_scale=code_scales[:, first:end],
                start=True,
                stop=True,
            )
            copy(results[b][:, first:end], acc[:, : end - first])

        def store(b, first, end):
            nc.sync.dma_start(out[b * P : (b + 1) * P, first:end], results[b][:, first:end])

        nc.vector.tensor_copy(grouped[1][:, :, 0], hid_early[:, PACK, :])
        nc.vector.tensor_copy(
            grouped[0][:].rearrange("p (c i) t -> p c t i", i=RUN),
            hid_early[:, 0:PACK, :].rearrange("p t (c i) -> p c t i", i=RUN),
        )
        quantise(0, HALF)
        nc.vector.tensor_copy(grouped[1][:, :, 1:LAST], hid_late[:, 0 : LAST - 1, :].rearrange("p t c -> p c t"))
        for first in range(0, HALF, P):
            nc.vector.tensor_copy(grouped[1][:, first : first + P, LAST], hid_late[:, LAST - 1, first : first + P])
        for first in range(HALF, O, P):
            quantise(first, first + P)
        for b in range(N // P):
            last_product(b, 0, HALF, b, nc.scalar.copy)
            store(b, 0, HALF)
        for piece, first in enumerate(range(HALF, O, P)):
            last_product(0, first, first + P, 2 + 2 * piece, nc.scalar.copy)
            last_product(1, first, first + P, 3 + 2 * piece, nc.vector.tensor_copy)
        for b in range(N // P):
            store(b, HALF, O)
